import numpy as np
import ml_dtypes


def mxq(x, axis, fmt="e4m3"):
    dtype, down = {"e4m3": (ml_dtypes.float8_e4m3fn, 7), "e5m2": (ml_dtypes.float8_e5m2, 14)}[fmt]
    v = np.moveaxis(np.asarray(x, np.float32).astype(ml_dtypes.bfloat16).astype(np.float64), axis, -1)
    blocks = v.reshape(v.shape[:-1] + (-1, 32))
    amax = np.abs(blocks).max(-1, keepdims=True)
    byte = np.maximum(np.where(amax > 0, np.frexp(amax)[1] - 1 + 127, 0) - down, 1)
    scale = np.exp2(byte - 127.0)
    codes = (blocks / scale).astype(np.float32).astype(dtype).astype(np.float64)
    return np.moveaxis((codes * scale).reshape(v.shape), -1, axis)


WIDE = False


def mx_kscale(k):
    if not WIDE:
        return np.ones(k)
    levels = np.array([10, -10, 5, -5, 0])
    if k % 512:
        return np.exp2(np.random.permutation(np.resize(levels, k // 32))).repeat(32)
    a = np.empty((k // 512, 16))
    for p in range(k // 512):
        a[p, :8] = np.random.permutation(np.resize(levels, 8))
        for g in range(8):
            far = levels[np.abs(levels - a[p, g]) >= 10]
            a[p, g + 8] = far[np.random.randint(len(far))]
    return np.exp2(a.ravel()).repeat(32)


def f64(x):
    return np.asarray(x).astype(np.float64)


def striped(idx):
    return np.tile(idx.reshape(-1, 16).T, (8, 1)).astype(np.uint16)


def unstriped(offs):
    return offs[:16].T.reshape(-1).astype(np.int64)


def striped8(idx):
    return np.concatenate([x.reshape(-1, 16).T for x in idx]).astype(np.uint16)


def runs(offs, k):
    lists = np.stack([offs[16 * r : 16 * r + 16].T.reshape(-1) for r in range(8)]).astype(np.int64)
    return lists[np.arange(k) % 512 // 64]


def pack_weight(w):
    k, n = w.shape
    w = f64(np.asarray(w, np.float32).astype(ml_dtypes.bfloat16)).reshape(k // 32, 32, n)
    amax = np.abs(w).max(1)
    byte = np.clip(np.where(amax > 0, np.frexp(amax)[1] - 1 + 127 - 7, 1), 1, 254)
    scaled = (w * np.exp2(127.0 - byte)[:, None, :]).reshape(k, n).astype(np.float32)
    words = np.ascontiguousarray(scaled.reshape(k // 512, 128, 4, n).transpose(0, 1, 3, 2)).astype(ml_dtypes.float8_e4m3fn).view(np.uint8)
    return words, np.ascontiguousarray(byte.astype(np.uint8).reshape(k // 512, 16, n))


def unpack_weight(words, scales):
    g, p, n, _ = words.shape
    vals = np.ascontiguousarray(words).view(ml_dtypes.float8_e4m3fn).astype(np.float64) * np.repeat(np.exp2(scales.astype(np.float64) - 127.0), 8, axis=1)[..., None]
    return vals.transpose(0, 1, 3, 2).reshape(g * 512, n)

def planes(y):
    n, m = y.shape
    v = y.astype(np.float32).astype(ml_dtypes.bfloat16).astype(np.float64).reshape(n // 32, 32, m)
    top = np.abs(v).max(1)
    byte = np.clip(np.where(top > 0, np.frexp(top)[1] - 1 + 127 - 7, 1), 1, 254)
    codes = (v * np.exp2(127.0 - byte)[:, None, :]).reshape(n, m).astype(np.float32).astype(ml_dtypes.float8_e4m3fn).view(np.uint8)
    words = codes.reshape(n // 512, 128, 4, m).transpose(0, 1, 3, 2)
    return np.ascontiguousarray(words), np.ascontiguousarray(byte.astype(np.uint8).reshape(n // 512, 16, m))


K, T, S, N, H, C = 512, 2048, 512, 512, 512, 512


def setup_inputs():
    n = np.random.standard_normal
    s = mx_kscale(K)[:, None]
    u = mx_kscale(S)
    packed_xT = pack_weight(n((K, T)) * s)
    packed_w1 = pack_weight(n((K, H)) / np.sqrt(K) / s)
    packed_w2 = pack_weight(n((H, N)) / np.sqrt(H) / u[:, None])
    return {
        "x_words": packed_xT[0],
        "x_scales": packed_xT[1],
        "w1_words": packed_w1[0],
        "w1_scales": packed_w1[1],
        "gn": (np.random.uniform(0.5, 1.5, (H, 1)) * u[:, None]).astype(np.float32),
        "w2_words": packed_w2[0],
        "w2_scales": packed_w2[1],
        "gs": (np.random.uniform(0.5, 1.5, (K, 1)) / s).astype(np.float32),
        "offs": striped(np.random.permutation(T)[:S]),
        "n1": striped8(np.stack([np.random.permutation(S) for _ in range(8)])),
        "n2": striped8(np.stack([np.random.permutation(S) for _ in range(8)])),
        "n3": striped8(np.stack([np.random.permutation(S) for _ in range(8)])),
        "n4": striped8(np.stack([np.random.permutation(S) for _ in range(8)])),
        "n5": striped8(np.stack([np.random.permutation(S) for _ in range(8)])),
        "cand": striped(np.random.permutation(T)[:C]),
        "n6": striped(np.random.permutation(S)),
        "n7": striped(np.random.permutation(S)),
    }


def reference(x_words, x_scales, w1_words, w1_scales, gn, w2_words, w2_scales, gs, offs, n1, n2, n3, n4, n5, cand, n6, n7):
    xq = unpack_weight(x_words, x_scales)[:, unstriped(offs)]
    y = unpack_weight(w1_words, w1_scales).T @ xq
    z = f64(gn) * (0.75 * (y * (y[np.arange(H)[:, None], runs(n1, H)]) + (y[np.arange(H)[:, None], runs(n2, H)]) * (y[np.arange(H)[:, None], runs(n3, H)])))
    a = unpack_weight(w2_words, w2_scales).T @ mxq(z, 0, "e4m3")
    x_cand = unpack_weight(x_words, x_scales)[:, unstriped(cand)]
    z2 = f64(gs) * (0.75 * ((y - (y[np.arange(H)[:, None], runs(n4, H)])) * (y - (y[np.arange(H)[:, None], runs(n5, H)]))))
    b = 0.0625 * ((x_cand.T @ mxq(z2, 0, "e4m3")))
    out_0 = a * (np.tanh(b[:, unstriped(n6)] - b[:, unstriped(n7)]))
    return (out_0,) + planes(out_0)

@@ -1,0 +1,208 @@
+from contextlib import ExitStack
+
+import concourse.mybir as mybir
+
+K, T, S = 512, 2048, 512
+FLOPS = 3 * 2 * 512 * 512 * 512
+
+F32 = mybir.dt.float32
+BF16 = mybir.dt.bfloat16
+I32 = mybir.dt.int32
+U32 = mybir.dt.uint32
+U16 = mybir.dt.uint16
+U8 = mybir.dt.uint8
+FP8X4 = mybir.dt.float8_e4m3fn_x4
+MULT = mybir.AluOpType.mult
+ADD = mybir.AluOpType.add
+SUB = mybir.AluOpType.subtract
+COPY = mybir.ActivationFunctionType.Copy
+TANH = mybir.ActivationFunctionType.Tanh
+
+P = 128
+PACK = 4
+HALF = S // 2
+HALVES = (0, 1)
+SLOTS = range(PACK)
+
+
+def tile_picked_fkcdjointbdotquad_none_po_kernel(
+    tc, x_words, x_scales, w1_words, w1_scales, gn, w2_words, w2_scales, gs,
+    offs, n1, n2, n3, n4, n5, cand, n6, n7, out_0, out_1, out_2,
+):
+    nc = tc.nc
+    with ExitStack() as ctx:
+        sb = ctx.enter_context(tc.tile_pool(name="sb", bufs=1))
+        ps = ctx.enter_context(tc.psum_pool(name="ps", bufs=1))
+
+        def new(name, shape, dtype):
+            return sb.tile(shape, dtype, name=name, align_bytes=64)
+
+        def load_list(name, src):
+            lst = new(name, [P, S // 16], U16)
+            nc.sync.dma_start(lst[:], src)
+            return lst
+
+        def load_words(queue, name, src, width):
+            words = new(name, [P, width], U32)
+            queue.dma_start(words[:].bitcast(I32), src[0].rearrange("p n t -> p (n t)").bitcast(I32))
+            return words
+
+        def zeroed_plane(name, width):
+            plane = new(name, [P, width], U8)
+            nc.vector.memset(plane[:].bitcast(I32), 0)
+            return plane
+
+        def load_scales(queue, plane, src):
+            for q in range(4):
+                queue.dma_start(plane[32 * q : 32 * q + 4, :].bitcast(I32), src[0, 4 * q : 4 * q + 4, :].bitcast(I32))
+
+        def dealt(ap):
+            return ap.rearrange("p (t m) -> p m t", t=PACK)
+
+        def in_order(ap):
+            return ap.rearrange("p (m t) -> p m t", t=PACK)
+
+        def deal(engine, name, words, plane):
+            words_d = new(name + "_words_dealt", [P, S], U32)
+            plane_d = new(name + "_scales_dealt", [P, S], U8)
+            engine.tensor_copy(dealt(words_d[:].bitcast(I32)), in_order(words[:].bitcast(I32)))
+            engine.tensor_copy(dealt(plane_d[:]), in_order(plane[:]))
+            return words_d, plane_d
+
+        def half_of(lst, h):
+            return lst[:, h * HALF // 16 : (h + 1) * HALF // 16]
+
+        def cols(h):
+            return slice(h * HALF, (h + 1) * HALF)
+
+        def product(bank, stat_words, stat_scales, t, mov_words, mov_scales):
+            m = slice(t * P, (t + 1) * P)
+            nc.tensor.matmul_mx(
+                out=bank, lhsT=stat_words[:, m].bitcast(FP8X4), lhsT_scale=stat_scales[:, m],
+                rhs=mov_words.bitcast(FP8X4), rhs_scale=mov_scales, start=True, stop=True,
+            )
+
+        def slots_read(planes):
+            return planes[:].rearrange("p t (c i) -> p c t i", i=4)
+
+        def slots_written(grouped):
+            return grouped[:].rearrange("p (c i) t -> p c t i", i=4)
+
+        def quantise(grouped, words, scales):
+            nc.vector.quantize_mx(out=words.bitcast(FP8X4), scales=scales, in_=grouped[:].rearrange("p j t -> p (j t)"))
+
+        xs = zeroed_plane("xs", T)
+        w1s = zeroed_plane("w1s", S)
+        w2s = zeroed_plane("w2s", S)
+        w1w = load_words(nc.sync, "w1w", w1_words, S)
+        load_scales(nc.sync, xs, x_scales)
+        offs_l = load_list("offs_l", offs)
+        xw = load_words(nc.sync, "xw", x_words, T)
+        load_scales(nc.sync, w1s, w1_scales)
+        cand_l = load_list("cand_l", cand)
+        gs_raw = new("gs_raw", [P, PACK], F32)
+        nc.sync.dma_start(gs_raw[:], gs.rearrange("(p t) o -> p (t o)", t=PACK))
+        gn_raw = new("gn_raw", [P, PACK], F32)
+        nc.sync.dma_start(gn_raw[:], gn.rearrange("(p t) o -> p (t o)", t=PACK))
+        n4_l = load_list("n4_l", n4)
+        n5_l = load_list("n5_l", n5)
+        n1_l = load_list("n1_l", n1)
+        n2_l = load_list("n2_l", n2)
+        n3_l = load_list("n3_l", n3)
+        w2w = load_words(nc.sync, "w2w", w2_words, S)
+        load_scales(nc.sync, w2s, w2_scales)
+        n7_l = load_list("n7_l", n7)
+        n6_l = load_list("n6_l", n6)
+
+        xq_s = new("xq_s", [P, S], U8)
+        nc.vector.tensor_copy(xq_s[:], xs[:].indirect(offs_l[:]))
+        w1w_d, w1s_d = deal(nc.vector, "w1", w1w, w1s)
+        xq_w = new("xq_w", [P, S], U32)
+        nc.vector.tensor_copy(xq_w[:], xw[:].indirect(offs_l[:]))
+        y_ps = [ps.tile([P, S], F32, name=f"y_ps{t}", tag=f"bank{t}") for t in SLOTS]
+        for t in SLOTS:
+            product(y_ps[t][:], w1w_d, w1s_d, t, xq_w[:], xq_s[:])
+
+        cw_d = new("cw_d", [P, S], U32)
+        nc.vector.tensor_copy(dealt(cw_d[:]), xw[:].indirect(cand_l[:]))
+        cs = new("cs", [P, S], U8)
+        nc.vector.tensor_copy(cs[:], xs[:].indirect(cand_l[:]))
+        gs75 = new("gs75", [P, PACK], F32)
+        nc.vector.tensor_scalar(gs75[:], gs_raw[:], 0.75, None, MULT)
+        gn75 = new("gn75", [P, PACK], F32)
+        nc.vector.tensor_scalar(gn75[:], gn_raw[:], 0.75, None, MULT)
+        cs_d = new("cs_d", [P, S], U8)
+        nc.vector.tensor_copy(dealt(cs_d[:]), in_order(cs[:]))
+        w2w_d, w2s_d = deal(nc.vector, "w2", w2w, w2s)
+
+        y = [new(f"y{t}", [P, S], F32) for t in SLOTS]
+        ys = [new(f"ys{t}", [P, S], F32) for t in SLOTS]
+        yn = [new(f"yn{t}", [P, S], F32) for t in SLOTS]
+
+        def planes(name):
+            return [new(f"{name}{h}", [P, PACK, HALF], F32) for h in HALVES]
+
+        g4, g5, d4, d5, g2, p1, p2 = (planes(n) for n in ("g4", "g5", "d4", "d5", "g2", "p1", "p2"))
+        g7, db, th, o = (planes(n) for n in ("g7", "db", "th", "o"))
+
+        def fetch(dst, window, lst, h):
+            nc.scalar.activation(dst, window[:].indirect(half_of(lst, h)), COPY)
+
+        def fetch_with(dst, window, lst, h, other, op):
+            nc.vector.tensor_tensor(dst, window[:].indirect(half_of(lst, h)), other, op)
+
+        z2_b = [new(f"z2_b{h}", [P, HALF, PACK], BF16) for h in HALVES]
+        z2_w = [new(f"z2_w{h}", [P, HALF], U32) for h in HALVES]
+        z2_s = [new(f"z2_s{h}", [P, HALF], U8) for h in HALVES]
+        b_ps = [ps.tile([P, S], F32, name=f"b_ps{t}") for t in SLOTS]
+        for h in HALVES:
+            for t in SLOTS:
+                if h == 0:
+                    nc.scalar.activation(y[t][:], y_ps[t][:], COPY)
+                    nc.scalar.activation(ys[t][:], y_ps[t][:], COPY, scale=gs75[:, t : t + 1])
+                    nc.vector.tensor_scalar(yn[t][:], y[t][:], gn75[:, t : t + 1], None, MULT)
+                fetch(g5[h][:, t, :], y[t], n5_l, h)
+                fetch(g4[h][:, t, :], ys[t], n4_l, h)
+                fetch_with(p1[h][:, t, :], y[t], n1_l, h, yn[t][:, cols(h)], MULT)
+                nc.vector.tensor_tensor(d5[h][:, t, :], y[t][:, cols(h)], g5[h][:, t, :], SUB)
+                nc.vector.tensor_tensor(d4[h][:, t, :], ys[t][:, cols(h)], g4[h][:, t, :], SUB)
+            nc.vector.tensor_tensor(slots_written(z2_b[h]), slots_read(d4[h]), slots_read(d5[h]), MULT)
+            quantise(z2_b[h], z2_w[h][:], z2_s[h][:])
+            for t in SLOTS:
+                product(b_ps[t][:, cols(h)], cw_d, cs_d, t, z2_w[h][:], z2_s[h][:])
+
+        z_b = [new(f"z_b{h}", [P, HALF, PACK], BF16) for h in HALVES]
+        z_w = [new(f"z_w{h}", [P, HALF], U32) for h in HALVES]
+        z_s = [new(f"z_s{h}", [P, HALF], U8) for h in HALVES]
+        a_ps = [ps.tile([P, S], F32, name=f"a_ps{t}", tag=f"bank{t}") for t in SLOTS]
+        b = [new(f"b{t}", [P, S], F32) for t in SLOTS]
+        for h in HALVES:
+            for t in SLOTS:
+                fetch(g2[h][:, t, :], yn[t], n2_l, h)
+                fetch_with(p2[h][:, t, :], y[t], n3_l, h, g2[h][:, t, :], MULT)
+            nc.vector.tensor_tensor(slots_written(z_b[h]), slots_read(p1[h]), slots_read(p2[h]), ADD)
+            quantise(z_b[h], z_w[h][:], z_s[h][:])
+            for t in SLOTS:
+                product(a_ps[t][:, cols(h)], w2w_d, w2s_d, t, z_w[h][:], z_s[h][:])
+
+        o_b = [new(f"o_b{h}", [P, HALF, PACK], BF16) for h in HALVES]
+        o_w = [new(f"o_w{h}", [P, HALF], U32) for h in HALVES]
+        o_s = new("o_s", [P, S], U8)
+        out_rows = out_0.rearrange("(p t) j -> p t j", t=PACK)
+        out_words = out_1[0].rearrange("p n t -> p (n t)").bitcast(I32)
+        for h in HALVES:
+            for t in SLOTS:
+                if h == 0:
+                    nc.scalar.activation(b[t][:], b_ps[t][:], COPY)
+                fetch(g7[h][:, t, :], b[t], n7_l, h)
+                fetch_with(db[h][:, t, :], b[t], n6_l, h, g7[h][:, t, :], SUB)
+        for h in HALVES:
+            for t in SLOTS:
+                nc.scalar.activation(th[h][:, t, :], db[h][:, t, :], TANH, scale=0.0625)
+                nc.vector.tensor_tensor(o[h][:, t, :], a_ps[t][:, cols(h)], th[h][:, t, :], MULT)
+            nc.sync.dma_start(out_rows[:, :, cols(h)], o[h][:])
+            nc.scalar.copy(slots_written(o_b[h]), slots_read(o[h]))
+            quantise(o_b[h], o_w[h][:], o_s[:, cols(h)])
+            nc.sync.dma_start(out_words[:, cols(h)], o_w[h][:].bitcast(I32))
+        for q in range(4):
+            nc.sync.dma_start(out_2[0, 4 * q : 4 * q + 4, :].bitcast(I32), o_s[32 * q : 32 * q + 4, :].bitcast(I32))

@@ -2,8 +2,9 @@ from contextlib import ExitStack
 
 import concourse.mybir as mybir
 
-K, T, S = 512, 2048, 512
-FLOPS = 3 * 2 * 512 * 512 * 512
+T = 2048
+S = 512
+FLOPS = 3 * 2 * S * S * S
 
 F32 = mybir.dt.float32
 BF16 = mybir.dt.bfloat16
@@ -20,9 +21,11 @@ TANH = mybir.ActivationFunctionType.Tanh
 
 P = 128
 PACK = 4
+SLOTS = range(PACK)
+LAST = PACK - 1
+QUADRANTS = range(4)
 HALF = S // 2
 HALVES = (0, 1)
-SLOTS = range(PACK)
 
 
 def tile_picked_fkcdjointbdotquad_none_po_kernel(
@@ -31,178 +34,214 @@ def tile_picked_fkcdjointbdotquad_none_po_kernel(
 ):
     nc = tc.nc
     with ExitStack() as ctx:
-        sb = ctx.enter_context(tc.tile_pool(name="sb", bufs=1))
-        ps = ctx.enter_context(tc.psum_pool(name="ps", bufs=1))
+        sbuf = ctx.enter_context(tc.tile_pool(name="sbuf", bufs=1))
+        psum = ctx.enter_context(tc.psum_pool(name="psum", bufs=1))
 
-        def new(name, shape, dtype):
-            return sb.tile(shape, dtype, name=name, align_bytes=64)
+        def new(name, shape, dtype, tag=""):
+            return sbuf.tile(shape, dtype, name=name, tag=tag, align_bytes=64)
 
         def load_list(name, src):
             lst = new(name, [P, S // 16], U16)
             nc.sync.dma_start(lst[:], src)
             return lst
 
-        def load_words(queue, name, src, width):
+        def load_gain(name, src):
+            gain = new(name, [P, PACK], F32)
+            nc.sync.dma_start(gain[:], src.rearrange("(p t) o -> p (t o)", t=PACK))
+            return gain
+
+        def load_words(name, src, width):
             words = new(name, [P, width], U32)
-            queue.dma_start(words[:].bitcast(I32), src[0].rearrange("p n t -> p (n t)").bitcast(I32))
+            nc.sync.dma_start(words[:].bitcast(I32), src[0].rearrange("p n t -> p (n t)").bitcast(I32))
             return words
 
-        def zeroed_plane(name, width):
-            plane = new(name, [P, width], U8)
-            nc.vector.memset(plane[:].bitcast(I32), 0)
-            return plane
+        def zeroed_scales(name, width):
+            scales = new(name, [P, width], U8)
+            nc.vector.memset(scales[:].bitcast(I32), 0)
+            return scales
 
-        def load_scales(queue, plane, src):
-            for q in range(4):
-                queue.dma_start(plane[32 * q : 32 * q + 4, :].bitcast(I32), src[0, 4 * q : 4 * q + 4, :].bitcast(I32))
+        def live_rows(scales, q):
+            return scales[32 * q : 32 * q + 4, :].bitcast(I32)
 
-        def dealt(ap):
-            return ap.rearrange("p (t m) -> p m t", t=PACK)
+        def load_scales(queues, scales, src):
+            for q in QUADRANTS:
+                queues[q // 2].dma_start(live_rows(scales, q), src[0, 4 * q : 4 * q + 4, :].bitcast(I32))
 
-        def in_order(ap):
-            return ap.rearrange("p (m t) -> p m t", t=PACK)
-
-        def deal(engine, name, words, plane):
-            words_d = new(name + "_words_dealt", [P, S], U32)
-            plane_d = new(name + "_scales_dealt", [P, S], U8)
-            engine.tensor_copy(dealt(words_d[:].bitcast(I32)), in_order(words[:].bitcast(I32)))
-            engine.tensor_copy(dealt(plane_d[:]), in_order(plane[:]))
-            return words_d, plane_d
-
-        def half_of(lst, h):
-            return lst[:, h * HALF // 16 : (h + 1) * HALF // 16]
+        def deal_on_write(dst, src):
+            nc.vector.tensor_copy(dst.rearrange("p (t m) -> p m t", t=PACK), src.rearrange("p (m t) -> p m t", t=PACK))
 
         def cols(h):
             return slice(h * HALF, (h + 1) * HALF)
 
-        def product(bank, stat_words, stat_scales, t, mov_words, mov_scales):
-            m = slice(t * P, (t + 1) * P)
-            nc.tensor.matmul_mx(
-                out=bank, lhsT=stat_words[:, m].bitcast(FP8X4), lhsT_scale=stat_scales[:, m],
-                rhs=mov_words.bitcast(FP8X4), rhs_scale=mov_scales, start=True, stop=True,
-            )
+        def looked_up(row, lst, h):
+            return row[:].indirect(lst[:, h * HALF // 16 : (h + 1) * HALF // 16])
 
-        def slots_read(planes):
-            return planes[:].rearrange("p t (c i) -> p c t i", i=4)
+        def slot_columns(words):
+            return [words[:, t * P : (t + 1) * P] for t in SLOTS]
 
-        def slots_written(grouped):
+        def products(banks, stat_words, stat_scales, mov_words, mov_scales):
+            for t in SLOTS:
+                m = slice(t * P, (t + 1) * P)
+                nc.tensor.matmul_mx(
+                    out=banks[t][:], lhsT=stat_words[t].bitcast(FP8X4), lhsT_scale=stat_scales[:, m],
+                    rhs=mov_words[:].bitcast(FP8X4), rhs_scale=mov_scales[:], start=True, stop=True,
+                )
+
+        def by_slots(values):
+            return values[:].rearrange("p t (c i) -> p c t i", i=4)
+
+        def side_by_side(grouped):
             return grouped[:].rearrange("p (c i) t -> p c t i", i=4)
 
         def quantise(grouped, words, scales):
             nc.vector.quantize_mx(out=words.bitcast(FP8X4), scales=scales, in_=grouped[:].rearrange("p j t -> p (j t)"))
 
-        xs = zeroed_plane("xs", T)
-        w1s = zeroed_plane("w1s", S)
-        w2s = zeroed_plane("w2s", S)
-        w1w = load_words(nc.sync, "w1w", w1_words, S)
-        load_scales(nc.sync, xs, x_scales)
+        xs = zeroed_scales("xs", T)
+        w1s = zeroed_scales("w1s", S)
+        w2s = zeroed_scales("w2s", S)
         offs_l = load_list("offs_l", offs)
-        xw = load_words(nc.sync, "xw", x_words, T)
-        load_scales(nc.sync, w1s, w1_scales)
+        load_scales((nc.sync, nc.scalar), xs, x_scales)
         cand_l = load_list("cand_l", cand)
-        gs_raw = new("gs_raw", [P, PACK], F32)
-        nc.sync.dma_start(gs_raw[:], gs.rearrange("(p t) o -> p (t o)", t=PACK))
-        gn_raw = new("gn_raw", [P, PACK], F32)
-        nc.sync.dma_start(gn_raw[:], gn.rearrange("(p t) o -> p (t o)", t=PACK))
-        n4_l = load_list("n4_l", n4)
+        xw = load_words("xw", x_words, T)
+        load_scales((nc.sync, nc.sync), w1s, w1_scales)
+        w1w = load_words("w1w", w1_words, S)
+        w2w = load_words("w2w", w2_words, S)
+        gs_t = load_gain("gs_t", gs)
+        gn_t = load_gain("gn_t", gn)
         n5_l = load_list("n5_l", n5)
+        n4_l = load_list("n4_l", n4)
         n1_l = load_list("n1_l", n1)
+        load_scales((nc.sync, nc.sync), w2s, w2_scales)
         n2_l = load_list("n2_l", n2)
         n3_l = load_list("n3_l", n3)
-        w2w = load_words(nc.sync, "w2w", w2_words, S)
-        load_scales(nc.sync, w2s, w2_scales)
         n7_l = load_list("n7_l", n7)
         n6_l = load_list("n6_l", n6)
 
         xq_s = new("xq_s", [P, S], U8)
         nc.vector.tensor_copy(xq_s[:], xs[:].indirect(offs_l[:]))
-        w1w_d, w1s_d = deal(nc.vector, "w1", w1w, w1s)
+        cand_s = new("cand_s", [P, S], U8)
+        nc.vector.tensor_copy(cand_s[:], xs[:].indirect(cand_l[:]))
         xq_w = new("xq_w", [P, S], U32)
         nc.vector.tensor_copy(xq_w[:], xw[:].indirect(offs_l[:]))
-        y_ps = [ps.tile([P, S], F32, name=f"y_ps{t}", tag=f"bank{t}") for t in SLOTS]
+        w1w_d = [new(f"w1w_d{t}", [P, P], U32) for t in SLOTS]
+        w1s_d = new("w1s_d", [P, S], U8)
+        nc.gpsimd.tensor_copy(w1s_d[:].rearrange("p (t m) -> p t m", t=PACK), w1s[:].rearrange("p (m t) -> p t m", t=PACK))
         for t in SLOTS:
-            product(y_ps[t][:], w1w_d, w1s_d, t, xq_w[:], xq_s[:])
+            nc.gpsimd.tensor_copy(w1w_d[t][:].bitcast(I32), w1w[:, t::PACK].bitcast(I32))
+        y_ps = [psum.tile([P, S], F32, name=f"y_ps{t}", tag=f"bank{t}") for t in SLOTS]
+        products(y_ps, [w[:] for w in w1w_d], w1s_d, xq_w, xq_s)
 
-        cw_d = new("cw_d", [P, S], U32)
-        nc.vector.tensor_copy(dealt(cw_d[:]), xw[:].indirect(cand_l[:]))
-        cs = new("cs", [P, S], U8)
-        nc.vector.tensor_copy(cs[:], xs[:].indirect(cand_l[:]))
-        gs75 = new("gs75", [P, PACK], F32)
-        nc.vector.tensor_scalar(gs75[:], gs_raw[:], 0.75, None, MULT)
-        gn75 = new("gn75", [P, PACK], F32)
-        nc.vector.tensor_scalar(gn75[:], gn_raw[:], 0.75, None, MULT)
-        cs_d = new("cs_d", [P, S], U8)
-        nc.vector.tensor_copy(dealt(cs_d[:]), in_order(cs[:]))
-        w2w_d, w2s_d = deal(nc.vector, "w2", w2w, w2s)
+        cand_wd = new("cand_wd", [P, S], U32)
+        nc.vector.tensor_copy(cand_wd[:].rearrange("p (t m) -> p m t", t=PACK), xw[:].indirect(cand_l[:]))
+        cand_sd = new("cand_sd", [P, S], U8, tag="xw")
+        deal_on_write(cand_sd[:], cand_s[:])
+        w2w_d = new("w2w_d", [P, S], U32)
+        w2s_d = new("w2s_d", [P, S], U8)
+        deal_on_write(w2w_d[:].bitcast(I32), w2w[:].bitcast(I32))
 
         y = [new(f"y{t}", [P, S], F32) for t in SLOTS]
         ys = [new(f"ys{t}", [P, S], F32) for t in SLOTS]
         yn = [new(f"yn{t}", [P, S], F32) for t in SLOTS]
-
-        def planes(name):
-            return [new(f"{name}{h}", [P, PACK, HALF], F32) for h in HALVES]
-
-        g4, g5, d4, d5, g2, p1, p2 = (planes(n) for n in ("g4", "g5", "d4", "d5", "g2", "p1", "p2"))
-        g7, db, th, o = (planes(n) for n in ("g7", "db", "th", "o"))
-
-        def fetch(dst, window, lst, h):
-            nc.scalar.activation(dst, window[:].indirect(half_of(lst, h)), COPY)
-
-        def fetch_with(dst, window, lst, h, other, op):
-            nc.vector.tensor_tensor(dst, window[:].indirect(half_of(lst, h)), other, op)
-
-        z2_b = [new(f"z2_b{h}", [P, HALF, PACK], BF16) for h in HALVES]
-        z2_w = [new(f"z2_w{h}", [P, HALF], U32) for h in HALVES]
-        z2_s = [new(f"z2_s{h}", [P, HALF], U8) for h in HALVES]
-        b_ps = [ps.tile([P, S], F32, name=f"b_ps{t}") for t in SLOTS]
-        for h in HALVES:
-            for t in SLOTS:
-                if h == 0:
-                    nc.scalar.activation(y[t][:], y_ps[t][:], COPY)
-                    nc.scalar.activation(ys[t][:], y_ps[t][:], COPY, scale=gs75[:, t : t + 1])
-                    nc.vector.tensor_scalar(yn[t][:], y[t][:], gn75[:, t : t + 1], None, MULT)
-                fetch(g5[h][:, t, :], y[t], n5_l, h)
-                fetch(g4[h][:, t, :], ys[t], n4_l, h)
-                fetch_with(p1[h][:, t, :], y[t], n1_l, h, yn[t][:, cols(h)], MULT)
-                nc.vector.tensor_tensor(d5[h][:, t, :], y[t][:, cols(h)], g5[h][:, t, :], SUB)
-                nc.vector.tensor_tensor(d4[h][:, t, :], ys[t][:, cols(h)], g4[h][:, t, :], SUB)
-            nc.vector.tensor_tensor(slots_written(z2_b[h]), slots_read(d4[h]), slots_read(d5[h]), MULT)
-            quantise(z2_b[h], z2_w[h][:], z2_s[h][:])
-            for t in SLOTS:
-                product(b_ps[t][:, cols(h)], cw_d, cs_d, t, z2_w[h][:], z2_s[h][:])
-
-        z_b = [new(f"z_b{h}", [P, HALF, PACK], BF16) for h in HALVES]
-        z_w = [new(f"z_w{h}", [P, HALF], U32) for h in HALVES]
-        z_s = [new(f"z_s{h}", [P, HALF], U8) for h in HALVES]
-        a_ps = [ps.tile([P, S], F32, name=f"a_ps{t}", tag=f"bank{t}") for t in SLOTS]
         b = [new(f"b{t}", [P, S], F32) for t in SLOTS]
-        for h in HALVES:
-            for t in SLOTS:
-                fetch(g2[h][:, t, :], yn[t], n2_l, h)
-                fetch_with(p2[h][:, t, :], y[t], n3_l, h, g2[h][:, t, :], MULT)
-            nc.vector.tensor_tensor(slots_written(z_b[h]), slots_read(p1[h]), slots_read(p2[h]), ADD)
-            quantise(z_b[h], z_w[h][:], z_s[h][:])
-            for t in SLOTS:
-                product(a_ps[t][:, cols(h)], w2w_d, w2s_d, t, z_w[h][:], z_s[h][:])
 
-        o_b = [new(f"o_b{h}", [P, HALF, PACK], BF16) for h in HALVES]
-        o_w = [new(f"o_w{h}", [P, HALF], U32) for h in HALVES]
-        o_s = new("o_s", [P, S], U8)
+        def four_slots(name, width=S, tag=""):
+            return new(name, [P, PACK, width], F32, tag=tag)
+
+        g4, g5, d4, d5, p1, p2 = (four_slots(name) for name in ("g4", "g5", "d4", "d5", "p1", "p2"))
+        g7, db, th, res = ([four_slots(f"{name}{h}", HALF) for h in HALVES] for name in ("g7", "db", "th", "res"))
+        z2_b, z2_w, z2_s = new("z2_b", [P, S, PACK], BF16), new("z2_w", [P, S], U32), new("z2_s", [P, S], U8)
+        z_b, z_w, z_s = new("z_b", [P, S, PACK], BF16), new("z_w", [P, S], U32), new("z_s", [P, S], U8)
+        res_w = [new(f"res_w{h}", [P, HALF], U32) for h in HALVES]
+        res_s = new("res_s", [P, S], U8)
+        b_ps = [psum.tile([P, S], F32, name=f"b_ps{t}") for t in SLOTS]
         out_rows = out_0.rearrange("(p t) j -> p t j", t=PACK)
         out_words = out_1[0].rearrange("p n t -> p (n t)").bitcast(I32)
-        for h in HALVES:
-            for t in SLOTS:
-                if h == 0:
-                    nc.scalar.activation(b[t][:], b_ps[t][:], COPY)
-                fetch(g7[h][:, t, :], b[t], n7_l, h)
-                fetch_with(db[h][:, t, :], b[t], n6_l, h, g7[h][:, t, :], SUB)
-        for h in HALVES:
-            for t in SLOTS:
-                nc.scalar.activation(th[h][:, t, :], db[h][:, t, :], TANH, scale=0.0625)
-                nc.vector.tensor_tensor(o[h][:, t, :], a_ps[t][:, cols(h)], th[h][:, t, :], MULT)
-            nc.sync.dma_start(out_rows[:, :, cols(h)], o[h][:])
-            nc.scalar.copy(slots_written(o_b[h]), slots_read(o[h]))
-            quantise(o_b[h], o_w[h][:], o_s[:, cols(h)])
-            nc.sync.dma_start(out_words[:, cols(h)], o_w[h][:].bitcast(I32))
-        for q in range(4):
-            nc.sync.dma_start(out_2[0, 4 * q : 4 * q + 4, :].bitcast(I32), o_s[32 * q : 32 * q + 4, :].bitcast(I32))
+
+        def fetch(dst, row, lst, h):
+            nc.scalar.activation(dst, looked_up(row, lst, h), COPY)
+
+        def fetch_row(dst, row, lst):
+            for h in HALVES:
+                fetch(dst[:, cols(h)], row, lst, h)
+
+        def fetch_row_times(dst, row, lst, other):
+            for h in HALVES:
+                nc.vector.tensor_tensor(dst[:, cols(h)], looked_up(row, lst, h), other[:, cols(h)], MULT)
+
+        def leave_bank(t):
+            nc.scalar.activation(y[t][:], y_ps[t][:], COPY)
+            nc.vector.tensor_scalar(ys[t][:], y[t][:], gs_t[:, t : t + 1], 0.75, MULT, MULT)
+            nc.vector.tensor_scalar(yn[t][:], y[t][:], gn_t[:, t : t + 1], 0.75, MULT, MULT)
+
+        leave_bank(0)
+        deal_on_write(w2s_d[:], w2s[:])
+        for t in SLOTS:
+            fetch_row(g5[:, t, :], y[t], n5_l)
+            fetch_row_times(p1[:, t, :], y[t], n1_l, yn[t])
+            if t < LAST:
+                leave_bank(t + 1)
+            fetch_row(g4[:, t, :], ys[t], n4_l)
+            nc.vector.tensor_tensor(d5[:, t, :], y[t][:], g5[:, t, :], SUB)
+            nc.vector.tensor_tensor(d4[:, t, :], ys[t][:], g4[:, t, :], SUB)
+
+        a_ps = [psum.tile([P, S], F32, name=f"a_ps{t}", tag=f"bank{t}") for t in SLOTS]
+        g3 = new("g3", [P, S], F32, tag=f"ys{LAST}")
+        g2 = four_slots("g2", tag=f"ys{LAST - 1}")
+        for t in SLOTS:
+            fetch_row(g2[:, t, :], yn[t], n2_l)
+        nc.vector.tensor_tensor(side_by_side(z2_b), by_slots(d4), by_slots(d5), MULT)
+        fetch_row_times(p2[:, 0, :], y[0], n3_l, g2[:, 0, :])
+        quantise(z2_b, z2_w[:], z2_s[:])
+        products(b_ps, slot_columns(cand_wd), cand_sd, z2_w, z2_s)
+        for t in range(1, LAST):
+            fetch_row_times(p2[:, t, :], y[t], n3_l, g2[:, t, :])
+        fetch_row(g3, y[LAST], n3_l)
+        nc.vector.tensor_tensor(p2[:, LAST, :], g2[:, LAST, :], g3[:], MULT)
+        for t in SLOTS:
+            nc.scalar.activation(b[t][:], b_ps[t][:], COPY)
+            fetch(g7[0][:, t, :], b[t], n7_l, 0)
+        nc.vector.tensor_tensor(side_by_side(z_b), by_slots(p1), by_slots(p2), ADD)
+        for t in SLOTS:
+            fetch(g7[1][:, t, :], b[t], n7_l, 1)
+
+        def difference(h, t):
+            nc.vector.tensor_tensor(db[h][:, t, :], looked_up(b[t], n6_l, h), g7[h][:, t, :], SUB)
+
+        def squash(h, slots):
+            nc.scalar.activation(th[h][:, slots, :], db[h][:, slots, :], TANH, scale=0.0625)
+
+        def result(h, t):
+            nc.vector.tensor_tensor(res[h][:, t, :], a_ps[t][:, cols(h)], th[h][:, t, :], MULT)
+            nc.sync.dma_start(out_rows[:, t, cols(h)], res[h][:, t, :])
+
+        def hand_on(h, grouped):
+            quantise(grouped, res_w[h][:], res_s[:, cols(h)])
+            nc.sync.dma_start(out_words[:, cols(h)], res_w[h][:].bitcast(I32))
+
+        difference(0, 0)
+        quantise(z_b, z_w[:], z_s[:])
+        products(a_ps, slot_columns(w2w_d), w2s_d, z_w, z_s)
+        for t in range(1, PACK):
+            difference(0, t)
+        squash(0, slice(0, 2))
+        squash(0, slice(2, 4))
+        g6 = new("g6", [P, HALF], F32)
+        for t in SLOTS:
+            if t < LAST:
+                difference(1, t)
+            else:
+                fetch(g6[:], b[t], n6_l, 1)
+                nc.vector.tensor_tensor(db[1][:, t, :], g6[:], g7[1][:, t, :], SUB)
+            result(0, t)
+            squash(1, slice(t, t + 1))
+        for t in SLOTS:
+            result(1, t)
+        res_b0 = new("res_b0", [P, HALF, PACK], BF16, tag="db1")
+        res_b1 = new("res_b1", [P, HALF, PACK], BF16)
+        nc.vector.tensor_copy(side_by_side(res_b1), by_slots(res[1]))
+        nc.scalar.copy(side_by_side(res_b0), by_slots(res[0]))
+        hand_on(1, res_b1)
+        hand_on(0, res_b0)
+        for q in QUADRANTS:
+            queue = nc.scalar if q < 3 else nc.sync
+            queue.dma_start(out_2[0, 4 * q : 4 * q + 4, :].bitcast(I32), live_rows(res_s, q))

from contextlib import ExitStack

import concourse.mybir as mybir

T = 2048
S = 512
FLOPS = 3 * 2 * S * S * S

F32 = mybir.dt.float32
BF16 = mybir.dt.bfloat16
I32 = mybir.dt.int32
U32 = mybir.dt.uint32
U16 = mybir.dt.uint16
U8 = mybir.dt.uint8
FP8X4 = mybir.dt.float8_e4m3fn_x4
MULT = mybir.AluOpType.mult
ADD = mybir.AluOpType.add
SUB = mybir.AluOpType.subtract
COPY = mybir.ActivationFunctionType.Copy
TANH = mybir.ActivationFunctionType.Tanh

P = 128
PACK = 4
SLOTS = range(PACK)
LAST = PACK - 1
QUADRANTS = range(4)
HALF = S // 2
HALVES = (0, 1)


def tile_picked_fkcdjointbdotquad_none_po_kernel(
    tc, x_words, x_scales, w1_words, w1_scales, gn, w2_words, w2_scales, gs,
    offs, n1, n2, n3, n4, n5, cand, n6, n7, out_0, out_1, out_2,
):
    nc = tc.nc
    with ExitStack() as ctx:
        sbuf = ctx.enter_context(tc.tile_pool(name="sbuf", bufs=1))
        psum = ctx.enter_context(tc.psum_pool(name="psum", bufs=1))

        def new(name, shape, dtype, tag=""):
            return sbuf.tile(shape, dtype, name=name, tag=tag, align_bytes=64)

        def load_list(name, src):
            lst = new(name, [P, S // 16], U16)
            nc.sync.dma_start(lst[:], src)
            return lst

        def load_gain(name, src):
            gain = new(name, [P, PACK], F32)
            nc.sync.dma_start(gain[:], src.rearrange("(p t) o -> p (t o)", t=PACK))
            return gain

        def load_words(name, src, width):
            words = new(name, [P, width], U32)
            nc.sync.dma_start(words[:].bitcast(I32), src[0].rearrange("p n t -> p (n t)").bitcast(I32))
            return words

        def zeroed_scales(name, width):
            scales = new(name, [P, width], U8)
            nc.vector.memset(scales[:].bitcast(I32), 0)
            return scales

        def live_rows(scales, q):
            return scales[32 * q : 32 * q + 4, :].bitcast(I32)

        def load_scales(queues, scales, src):
            for q in QUADRANTS:
                queues[q // 2].dma_start(live_rows(scales, q), src[0, 4 * q : 4 * q + 4, :].bitcast(I32))

        def deal_on_write(dst, src):
            nc.vector.tensor_copy(dst.rearrange("p (t m) -> p m t", t=PACK), src.rearrange("p (m t) -> p m t", t=PACK))

        def cols(h):
            return slice(h * HALF, (h + 1) * HALF)

        def looked_up(row, lst, h):
            return row[:].indirect(lst[:, h * HALF // 16 : (h + 1) * HALF // 16])

        def slot_columns(words):
            return [words[:, t * P : (t + 1) * P] for t in SLOTS]

        def products(banks, stat_words, stat_scales, mov_words, mov_scales):
            for t in SLOTS:
                m = slice(t * P, (t + 1) * P)
                nc.tensor.matmul_mx(
                    out=banks[t][:], lhsT=stat_words[t].bitcast(FP8X4), lhsT_scale=stat_scales[:, m],
                    rhs=mov_words[:].bitcast(FP8X4), rhs_scale=mov_scales[:], start=True, stop=True,
                )

        def by_slots(values):
            return values[:].rearrange("p t (c i) -> p c t i", i=4)

        def side_by_side(grouped):
            return grouped[:].rearrange("p (c i) t -> p c t i", i=4)

        def quantise(grouped, words, scales):
            nc.vector.quantize_mx(out=words.bitcast(FP8X4), scales=scales, in_=grouped[:].rearrange("p j t -> p (j t)"))

        xs = zeroed_scales("xs", T)
        w1s = zeroed_scales("w1s", S)
        w2s = zeroed_scales("w2s", S)
        offs_l = load_list("offs_l", offs)
        load_scales((nc.sync, nc.scalar), xs, x_scales)
        cand_l = load_list("cand_l", cand)
        xw = load_words("xw", x_words, T)
        load_scales((nc.sync, nc.sync), w1s, w1_scales)
        w1w = load_words("w1w", w1_words, S)
        w2w = load_words("w2w", w2_words, S)
        gs_t = load_gain("gs_t", gs)
        gn_t = load_gain("gn_t", gn)
        n5_l = load_list("n5_l", n5)
        n4_l = load_list("n4_l", n4)
        n1_l = load_list("n1_l", n1)
        load_scales((nc.sync, nc.sync), w2s, w2_scales)
        n2_l = load_list("n2_l", n2)
        n3_l = load_list("n3_l", n3)
        n7_l = load_list("n7_l", n7)
        n6_l = load_list("n6_l", n6)

        xq_s = new("xq_s", [P, S], U8)
        nc.vector.tensor_copy(xq_s[:], xs[:].indirect(offs_l[:]))
        cand_s = new("cand_s", [P, S], U8)
        nc.vector.tensor_copy(cand_s[:], xs[:].indirect(cand_l[:]))
        xq_w = new("xq_w", [P, S], U32)
        nc.vector.tensor_copy(xq_w[:], xw[:].indirect(offs_l[:]))
        w1w_d = [new(f"w1w_d{t}", [P, P], U32) for t in SLOTS]
        w1s_d = new("w1s_d", [P, S], U8)
        nc.gpsimd.tensor_copy(w1s_d[:].rearrange("p (t m) -> p t m", t=PACK), w1s[:].rearrange("p (m t) -> p t m", t=PACK))
        for t in SLOTS:
            nc.gpsimd.tensor_copy(w1w_d[t][:].bitcast(I32), w1w[:, t::PACK].bitcast(I32))
        y_ps = [psum.tile([P, S], F32, name=f"y_ps{t}", tag=f"bank{t}") for t in SLOTS]
        products(y_ps, [w[:] for w in w1w_d], w1s_d, xq_w, xq_s)

        cand_wd = new("cand_wd", [P, S], U32)
        nc.vector.tensor_copy(cand_wd[:].rearrange("p (t m) -> p m t", t=PACK), xw[:].indirect(cand_l[:]))
        cand_sd = new("cand_sd", [P, S], U8, tag="xw")
        deal_on_write(cand_sd[:], cand_s[:])
        w2w_d = new("w2w_d", [P, S], U32)
        w2s_d = new("w2s_d", [P, S], U8)
        deal_on_write(w2w_d[:].bitcast(I32), w2w[:].bitcast(I32))

        y = [new(f"y{t}", [P, S], F32) for t in SLOTS]
        ys = [new(f"ys{t}", [P, S], F32) for t in SLOTS]
        yn = [new(f"yn{t}", [P, S], F32) for t in SLOTS]
        b = [new(f"b{t}", [P, S], F32) for t in SLOTS]

        def four_slots(name, width=S, tag=""):
            return new(name, [P, PACK, width], F32, tag=tag)

        g4, g5, d4, d5, p1, p2 = (four_slots(name) for name in ("g4", "g5", "d4", "d5", "p1", "p2"))
        g7, db, th, res = ([four_slots(f"{name}{h}", HALF) for h in HALVES] for name in ("g7", "db", "th", "res"))
        z2_b, z2_w, z2_s = new("z2_b", [P, S, PACK], BF16), new("z2_w", [P, S], U32), new("z2_s", [P, S], U8)
        z_b, z_w, z_s = new("z_b", [P, S, PACK], BF16), new("z_w", [P, S], U32), new("z_s", [P, S], U8)
        res_w = [new(f"res_w{h}", [P, HALF], U32) for h in HALVES]
        res_s = new("res_s", [P, S], U8)
        b_ps = [psum.tile([P, S], F32, name=f"b_ps{t}") for t in SLOTS]
        out_rows = out_0.rearrange("(p t) j -> p t j", t=PACK)
        out_words = out_1[0].rearrange("p n t -> p (n t)").bitcast(I32)

        def fetch(dst, row, lst, h):
            nc.scalar.activation(dst, looked_up(row, lst, h), COPY)

        def fetch_row(dst, row, lst):
            for h in HALVES:
                fetch(dst[:, cols(h)], row, lst, h)

        def fetch_row_times(dst, row, lst, other):
            for h in HALVES:
                nc.vector.tensor_tensor(dst[:, cols(h)], looked_up(row, lst, h), other[:, cols(h)], MULT)

        def leave_bank(t):
            nc.scalar.activation(y[t][:], y_ps[t][:], COPY)
            nc.vector.tensor_scalar(ys[t][:], y[t][:], gs_t[:, t : t + 1], 0.75, MULT, MULT)
            nc.vector.tensor_scalar(yn[t][:], y[t][:], gn_t[:, t : t + 1], 0.75, MULT, MULT)

        leave_bank(0)
        deal_on_write(w2s_d[:], w2s[:])
        for t in SLOTS:
            fetch_row(g5[:, t, :], y[t], n5_l)
            fetch_row_times(p1[:, t, :], y[t], n1_l, yn[t])
            if t < LAST:
                leave_bank(t + 1)
            fetch_row(g4[:, t, :], ys[t], n4_l)
            nc.vector.tensor_tensor(d5[:, t, :], y[t][:], g5[:, t, :], SUB)
            nc.vector.tensor_tensor(d4[:, t, :], ys[t][:], g4[:, t, :], SUB)

        a_ps = [psum.tile([P, S], F32, name=f"a_ps{t}", tag=f"bank{t}") for t in SLOTS]
        g3 = new("g3", [P, S], F32, tag=f"ys{LAST}")
        g2 = four_slots("g2", tag=f"ys{LAST - 1}")
        for t in SLOTS:
            fetch_row(g2[:, t, :], yn[t], n2_l)
        nc.vector.tensor_tensor(side_by_side(z2_b), by_slots(d4), by_slots(d5), MULT)
        fetch_row_times(p2[:, 0, :], y[0], n3_l, g2[:, 0, :])
        quantise(z2_b, z2_w[:], z2_s[:])
        products(b_ps, slot_columns(cand_wd), cand_sd, z2_w, z2_s)
        for t in range(1, LAST):
            fetch_row_times(p2[:, t, :], y[t], n3_l, g2[:, t, :])
        fetch_row(g3, y[LAST], n3_l)
        nc.vector.tensor_tensor(p2[:, LAST, :], g2[:, LAST, :], g3[:], MULT)
        for t in SLOTS:
            nc.scalar.activation(b[t][:], b_ps[t][:], COPY)
            fetch(g7[0][:, t, :], b[t], n7_l, 0)
        nc.vector.tensor_tensor(side_by_side(z_b), by_slots(p1), by_slots(p2), ADD)
        for t in SLOTS:
            fetch(g7[1][:, t, :], b[t], n7_l, 1)

        def difference(h, t):
            nc.vector.tensor_tensor(db[h][:, t, :], looked_up(b[t], n6_l, h), g7[h][:, t, :], SUB)

        def squash(h, slots):
            nc.scalar.activation(th[h][:, slots, :], db[h][:, slots, :], TANH, scale=0.0625)

        def result(h, t):
            nc.vector.tensor_tensor(res[h][:, t, :], a_ps[t][:, cols(h)], th[h][:, t, :], MULT)
            nc.sync.dma_start(out_rows[:, t, cols(h)], res[h][:, t, :])

        def hand_on(h, grouped):
            quantise(grouped, res_w[h][:], res_s[:, cols(h)])
            nc.sync.dma_start(out_words[:, cols(h)], res_w[h][:].bitcast(I32))

        difference(0, 0)
        quantise(z_b, z_w[:], z_s[:])
        products(a_ps, slot_columns(w2w_d), w2s_d, z_w, z_s)
        for t in range(1, PACK):
            difference(0, t)
        squash(0, slice(0, 2))
        squash(0, slice(2, 4))
        g6 = new("g6", [P, HALF], F32)
        for t in SLOTS:
            if t < LAST:
                difference(1, t)
            else:
                fetch(g6[:], b[t], n6_l, 1)
                nc.vector.tensor_tensor(db[1][:, t, :], g6[:], g7[1][:, t, :], SUB)
            result(0, t)
            squash(1, slice(t, t + 1))
        for t in SLOTS:
            result(1, t)
        res_b0 = new("res_b0", [P, HALF, PACK], BF16, tag="db1")
        res_b1 = new("res_b1", [P, HALF, PACK], BF16)
        nc.vector.tensor_copy(side_by_side(res_b1), by_slots(res[1]))
        nc.scalar.copy(side_by_side(res_b0), by_slots(res[0]))
        hand_on(1, res_b1)
        hand_on(0, res_b0)
        for q in QUADRANTS:
            queue = nc.scalar if q < 3 else nc.sync
            queue.dma_start(out_2[0, 4 * q : 4 * q + 4, :].bitcast(I32), live_rows(res_s, q))
